import numpy as np
import ml_dtypes


def mxq(x, axis, fmt="e4m3"):
    dtype, down = {"e4m3": (ml_dtypes.float8_e4m3fn, 7), "e5m2": (ml_dtypes.float8_e5m2, 14)}[fmt]
    v = np.moveaxis(np.asarray(x, np.float32).astype(ml_dtypes.bfloat16).astype(np.float64), axis, -1)
    blocks = v.reshape(v.shape[:-1] + (-1, 32))
    amax = np.abs(blocks).max(-1, keepdims=True)
    byte = np.maximum(np.where(amax > 0, np.frexp(amax)[1] - 1 + 127, 0) - down, 1)
    scale = np.exp2(byte - 127.0)
    codes = (blocks / scale).astype(np.float32).astype(dtype).astype(np.float64)
    return np.moveaxis((codes * scale).reshape(v.shape), -1, axis)


WIDE = False


def mx_kscale(k):
    if not WIDE:
        return np.ones(k)
    levels = np.array([10, -10, 5, -5, 0])
    if k % 512:
        return np.exp2(np.random.permutation(np.resize(levels, k // 32))).repeat(32)
    a = np.empty((k // 512, 16))
    for p in range(k // 512):
        a[p, :8] = np.random.permutation(np.resize(levels, 8))
        for g in range(8):
            far = levels[np.abs(levels - a[p, g]) >= 10]
            a[p, g + 8] = far[np.random.randint(len(far))]
    return np.exp2(a.ravel()).repeat(32)


def f64(x):
    return np.asarray(x).astype(np.float64)


def striped(idx):
    return np.tile(idx.reshape(-1, 16).T, (8, 1)).astype(np.uint16)


def unstriped(offs):
    return offs[:16].T.reshape(-1).astype(np.int64)


E2M1 = np.array([0.0, 0.5, 1.0, 1.5, 2.0, 3.0, 4.0, 6.0, -0.0, -0.5, -1.0, -1.5, -2.0, -3.0, -4.0, -6.0])


def pack_weight(w, fmt):
    k, n = w.shape
    w = f64(np.asarray(w, np.float32).astype(ml_dtypes.bfloat16)).reshape(k // 32, 32, n)
    amax = np.abs(w).max(1)
    if fmt == "e4m3":
        byte = np.frexp(amax)[1] - 1 + 127 - 7
    else:
        mant, ex = np.frexp(amax / 6.0)
        byte = np.where(mant > 0.5, ex, ex - 1) + 127
    byte = np.clip(np.where(amax > 0, byte, 1), 1, 254)
    scaled = (w * np.exp2(127.0 - byte)[:, None, :]).reshape(k, n).astype(np.float32)
    by_word = np.ascontiguousarray(scaled.reshape(k // 512, 128, 4, n).transpose(0, 1, 3, 2))
    if fmt == "e4m3":
        words = by_word.astype(ml_dtypes.float8_e4m3fn).view(np.uint8)
    else:
        c = by_word.astype(ml_dtypes.float4_e2m1fn).view(np.uint8) & 0xF
        words = (c[..., 0::2] | (c[..., 1::2] << 4)).reshape(k // 512, 128, 2 * n)
    return np.ascontiguousarray(words), np.ascontiguousarray(byte.astype(np.uint8).reshape(k // 512, 16, n))


def unpack_weight(words, scales, fmt):
    g, _, n = scales.shape
    words = np.ascontiguousarray(words).reshape(g, 128, n, -1)
    if fmt == "e4m3":
        vals = words.view(ml_dtypes.float8_e4m3fn).astype(np.float64)
    else:
        nib = np.empty((g, 128, n, 4), np.uint8)
        nib[..., 0::2] = words & 0xF
        nib[..., 1::2] = words >> 4
        vals = E2M1[nib]
    vals = vals * np.repeat(np.exp2(scales.astype(np.float64) - 127.0), 8, axis=1)[..., None]
    return vals.transpose(0, 1, 3, 2).reshape(g * 512, n)


def gelu(v):
    return 0.5 * v * (1.0 + np.tanh(np.sqrt(2.0 / np.pi) * (v + 0.044715 * v**3)))


def bf(x):
    return np.asarray(x, np.float32).astype(ml_dtypes.bfloat16)


def planes(Y):
    n, m = Y.shape
    b = f64(bf(Y)).reshape(n // 32, 32, m)
    amax = np.abs(b).max(1)
    byte = np.clip(np.where(amax > 0, np.frexp(amax)[1] - 1 + 127 - 7, 1), 1, 254)
    codes = (b * np.exp2(127.0 - byte)[:, None, :]).reshape(n, m).astype(np.float32).astype(ml_dtypes.float8_e4m3fn).view(np.uint8)
    words = codes.reshape(n // 512, 128, 4, m).transpose(0, 1, 3, 2)
    return np.ascontiguousarray(words), np.ascontiguousarray(byte.astype(np.uint8).reshape(n // 512, 16, m))


T, S, K, H, P1, P2, P3, N = 4096, 2048, 1024, 512, 1024, 512, 256, 1024


def setup_inputs():
    n = np.random.standard_normal
    s = mx_kscale(K)[:, None]
    u = mx_kscale(H)[:, None]
    tab_words, tab_scales = pack_weight(n((K, T)) * s, "e4m3")
    wt = (1.3 * n((K, H)) / np.sqrt(K) / s).astype(np.float32)
    wc_words, wc_scales = pack_weight(0.5 * n((K, H)) / np.sqrt(K) / s, "e2m1")
    gain = (2.0 * np.exp(0.3 * n(H)) * u[:, 0]).astype(np.float32)
    wl = (n((H, N)) / np.sqrt(H) / u * np.exp(0.8 * n(N))).astype(np.float32)
    draw1 = np.random.permutation(S)
    draw2 = np.random.permutation(P1)
    draw3 = np.random.permutation(P2)
    return {"tab_words": tab_words, "tab_scales": tab_scales, "wt": wt,
            "wc_words": wc_words, "wc_scales": wc_scales, "gain": gain, "wl": wl,
            "offs": striped(np.random.permutation(T)[:S]),
            "pos1": striped(draw1[:P1]), "pos2": striped(draw1[P1:]),
            "pos3": striped(draw2[:P2]), "pos4": striped(draw2[P2:]),
            "pos5": striped(draw3[:P3]), "pos6": striped(draw3[P3:])}


def reference(tab_words, tab_scales, wt, wc_words, wc_scales, gain, wl,
              offs, pos1, pos2, pos3, pos4, pos5, pos6):
    v = unpack_weight(tab_words, tab_scales, "e4m3")[:, unstriped(offs)]
    tone = mxq(f64(wt), 0, "e4m3").T @ v
    phase = unpack_weight(wc_words, wc_scales, "e2m1").T @ v
    h = np.tanh(tone) * np.cos(phase)
    a1 = np.maximum(h[:, unstriped(pos1)], h[:, unstriped(pos2)])
    a2 = a1[:, unstriped(pos3)] - a1[:, unstriped(pos4)]
    a3 = a2[:, unstriped(pos5)] * a2[:, unstriped(pos6)] * f64(gain)[:, None]
    y = mxq(f64(wl), 0, "e4m3").T @ mxq(a3, 0, "e4m3")
    words, scales = planes(y)
    return y, words, scales

@@ -1,0 +1,282 @@
+import math
+from contextlib import ExitStack
+
+import concourse.mybir as mybir
+
+T, S, K, H, P1, P2, P3, N = 4096, 2048, 1024, 512, 1024, 512, 256, 1024
+FLOPS = 2 * (2 * K * H * S + H * N * P3)
+
+F32 = mybir.dt.float32
+BF16 = mybir.dt.bfloat16
+I32 = mybir.dt.int32
+U32 = mybir.dt.uint32
+U16 = mybir.dt.uint16
+U8 = mybir.dt.uint8
+FP8X4 = mybir.dt.float8_e4m3fn_x4
+FP4X4 = mybir.dt.float4_e2m1fn_x4
+ALU = mybir.AluOpType
+ACT = mybir.ActivationFunctionType
+
+P = 128
+PACK = 4
+PASSES = K // (P * PACK)
+BANK = 512
+CHUNK = 1024
+GROUPS = N // (P * PACK)
+TWO_PI = 2.0 * math.pi
+
+
+def tile_list_blind_audition_heats_kernel(
+    tc, tab_words, tab_scales, wt, wc_words, wc_scales, gain, wl,
+    offs, pos1, pos2, pos3, pos4, pos5, pos6, out_0, out_1, out_2,
+):
+    nc = tc.nc
+    with ExitStack() as ctx:
+        keep = ctx.enter_context(tc.tile_pool(name="keep", bufs=1))
+        big = ctx.enter_context(tc.tile_pool(name="big", bufs=2))
+        work = ctx.enter_context(tc.tile_pool(name="work", bufs=2))
+        psum = ctx.enter_context(tc.psum_pool(name="psum", bufs=8))
+
+        def load_list(name, src):
+            tile = keep.tile(list(src.shape), U16, name=name)
+            nc.sync.dma_start(tile[:], src)
+            return tile
+
+        offs_sb = load_list("offs_sb", offs)
+
+        scale_win = keep.tile([P, T], U8)
+        nc.sync.dma_start(
+            scale_win[96:P, :].bitcast(I32),
+            tab_scales.bitcast(I32).rearrange("a q w -> q a w"),
+        )
+        nc.vector.memset(scale_win[0:96, :].bitcast(I32), 0)
+
+        word_win = []
+        for a in range(PASSES):
+            win = big.tile([P, T], I32, tag="big", name=f"word_win{a}")
+            nc.sync.dma_start(win[:], tab_words[a].rearrange("p t i -> p (t i)").bitcast(I32))
+            word_win.append(win)
+
+        zero_in = keep.tile([P, 1], F32)
+        zero_bias = keep.tile([P, 1], F32)
+        nc.gpsimd.memset(zero_in[:], 0.0)
+        nc.scalar.activation(zero_bias[:], zero_in[:], ACT.Silu)
+
+        wcs_raw = keep.tile([P, PASSES, H], U8)
+        nc.gpsimd.memset(wcs_raw[:].bitcast(I32), 0)
+        for q in range(4):
+            nc.scalar.dma_start(
+                wcs_raw[32 * q:32 * q + 4].bitcast(I32),
+                wc_scales[:, 4 * q:4 * q + 4, :].bitcast(I32).rearrange("a r w -> r a w"),
+            )
+
+        wc_raw = keep.tile([P, PASSES, 2 * H], U8)
+        nc.sync.dma_start(wc_raw[:].bitcast(I32), wc_words.bitcast(I32).rearrange("a p w -> p a w"))
+
+        wt_raw = []
+        for a in range(PASSES):
+            raw = keep.tile([P, PACK, H], F32, name=f"wt_raw{a}")
+            nc.sync.dma_start(raw[:], wt[a * 512:(a + 1) * 512, :].rearrange("(p j) c -> p j c", j=PACK))
+            wt_raw.append(raw)
+
+        pos = [load_list("pos_sb0", pos1)]
+
+        v_scales = keep.tile([P, PASSES * S], U8, align_bytes=64)
+        nc.gpsimd.memset(v_scales[:].bitcast(I32), 0)
+        picked_scales = keep.tile([P, S], U8)
+        nc.vector.tensor_copy(picked_scales[:], scale_win[:].indirect(offs_sb[:]))
+        for q in range(4):
+            nc.scalar.dma_start(
+                v_scales[32 * q:32 * q + 4, :].bitcast(I32),
+                picked_scales[96 + 8 * q:96 + 8 * q + 8, :].bitcast(I32),
+            )
+        pos.extend(load_list(f"pos_sb{i + 1}", src) for i, src in enumerate((pos2, pos3, pos4, pos5, pos6)))
+
+        v_words = [keep.tile([P, S], U32, align_bytes=64, name=f"v_words{a}") for a in range(PASSES)]
+        nc.vector.tensor_copy(v_words[0][:], word_win[0][:].bitcast(U32).indirect(offs_sb[:]))
+
+        wc_codes = keep.tile([P, PASSES, PACK, 2 * P], U8, align_bytes=64)
+        wc_planes = keep.tile([P, PASSES, PACK, P], U8, align_bytes=64)
+        nc.vector.tensor_copy(
+            wc_planes[:].bitcast(I32).rearrange("p a t (q w) -> p a t q w", w=2),
+            wcs_raw[:].bitcast(I32).rearrange("p a (q t w) -> p a t q w", t=PACK, w=2),
+        )
+        for s in range(S // BANK):
+            nc.vector.tensor_copy(
+                v_words[1][:, s * BANK:(s + 1) * BANK],
+                word_win[1][:].bitcast(U32).indirect(offs_sb[:, s * BANK // 16:(s + 1) * BANK // 16]),
+            )
+            if s == 0:
+                nc.vector.tensor_copy(
+                    wc_codes[:].bitcast(I32).rearrange("p a t (q w) -> p a t q w", w=4),
+                    wc_raw[:].bitcast(I32).rearrange("p a (q t w) -> p a t q w", t=PACK, w=4),
+                )
+
+        wt_codes, wt_planes = [], []
+
+        def quantise_wt(t):
+            rounded = keep.tile([P, PASSES, P, PACK], BF16, align_bytes=64, name=f"wt_bf{t}")
+            for a in range(PASSES):
+                nc.scalar.copy(
+                    rounded[:, a].rearrange("p (q s) j -> p q s j", s=8),
+                    wt_raw[a][:].rearrange("p j (q t s) -> p t q s j", t=PACK, s=8)[:, t],
+                )
+            codes = keep.tile([P, PASSES * P], U32, align_bytes=64, name=f"wt_codes{t}")
+            plane = keep.tile([P, PASSES * P], U8, align_bytes=64, name=f"wt_plane{t}")
+            nc.vector.quantize_mx(
+                out=codes[:].bitcast(FP8X4), scales=plane[:],
+                in_=rounded[:].rearrange("p a m j -> p (a m j)"),
+            )
+            wt_codes.append(codes)
+            wt_planes.append(plane)
+
+        def product(codes, planes, s):
+            bank = psum.tile([P, BANK], F32, tag="bank", name="bank")
+            for a in range(PASSES):
+                nc.tensor.matmul_mx(
+                    out=bank[:], lhsT=codes[a], lhsT_scale=planes[a],
+                    rhs=v_words[a][:, s * BANK:(s + 1) * BANK].bitcast(FP8X4),
+                    rhs_scale=v_scales[:, a * S + s * BANK:a * S + (s + 1) * BANK],
+                    start=(a == 0), stop=(a == PASSES - 1),
+                )
+            return bank
+
+        angles = {}
+
+        def reduce_phase(t):
+            codes = [wc_codes[:, a, t, :].bitcast(FP4X4) for a in range(PASSES)]
+            planes = [wc_planes[:, a, t, :] for a in range(PASSES)]
+            for c in range(S // CHUNK):
+                angle = work.tile([P, CHUNK], F32, tag="angle", name="angle", bufs=6)
+                turns = work.tile([P, CHUNK], U32, tag="turns", name="turns", bufs=4)
+                for i in range(CHUNK // BANK):
+                    bank = product(codes, planes, c * CHUNK // BANK + i)
+                    nc.scalar.activation(angle[:, i * BANK:(i + 1) * BANK], bank[:], ACT.Abs)
+                nc.scalar.activation(turns[:], angle[:], ACT.Copy, scale=1.0 / TWO_PI, bias=-0.25)
+                nc.vector.scalar_tensor_tensor(
+                    angle[:], turns[:].bitcast(I32), TWO_PI, angle[:], ALU.mult, ALU.subtract,
+                )
+                angles[t, c] = angle
+
+        def features(t):
+            h = work.tile([P, S], F32, tag="h", name="h")
+            codes = [wt_codes[t][:, a * P:(a + 1) * P].bitcast(FP8X4) for a in range(PASSES)]
+            planes = [wt_planes[t][:, a * P:(a + 1) * P] for a in range(PASSES)]
+            for c in range(S // CHUNK):
+                tanh_tone = work.tile([P, CHUNK], F32, tag="tanh_tone", name="tanh_tone", bufs=4)
+                for i in range(CHUNK // BANK):
+                    bank = product(codes, planes, c * CHUNK // BANK + i)
+                    nc.scalar.activation(tanh_tone[:, i * BANK:(i + 1) * BANK], bank[:], ACT.Tanh, bias=zero_bias[:])
+                angle = angles[t, c]
+                nc.scalar.activation(angle[:], angle[:], ACT.Sin, bias=math.pi / 2)
+                nc.vector.tensor_tensor(h[:, c * CHUNK:(c + 1) * CHUNK], tanh_tone[:], angle[:], ALU.mult)
+            return h
+
+        gain_col = [keep.tile([P, 1], F32, name=f"gain_col{t}") for t in range(PACK)]
+        gain_rows = keep.tile([P, PACK, P3], F32)
+        a3 = keep.tile([P, PACK, P3], F32)
+
+        def levels(t, h):
+            left = work.tile([P, P1], F32, tag="left1", name="left1", bufs=1)
+            right = work.tile([P, P1], F32, tag="right1", name="right1", bufs=1)
+            a1 = work.tile([P, P1], F32, tag="a1", name="a1", bufs=1)
+            nc.vector.tensor_copy(left[:], h[:].indirect(pos[0][:]))
+            nc.vector.tensor_copy(right[:], h[:].indirect(pos[1][:]))
+            nc.vector.tensor_tensor(a1[:], left[:], right[:], ALU.max)
+            right2 = work.tile([P, P2], F32, tag="right2", name="right2", bufs=1)
+            a2 = work.tile([P, P2], F32, tag="a2", name="a2", bufs=1)
+            nc.vector.tensor_copy(right2[:], a1[:].indirect(pos[3][:]))
+            nc.vector.tensor_tensor(a2[:], a1[:].indirect(pos[2][:]), right2[:], ALU.subtract)
+            left3 = work.tile([P, P3], F32, tag="left3", name="left3", bufs=1)
+            nc.vector.tensor_tensor(left3[:], a2[:].indirect(pos[4][:]), gain_rows[:, t, :], ALU.mult)
+            nc.vector.tensor_tensor(a3[:, t, :], a2[:].indirect(pos[5][:]), left3[:], ALU.mult)
+
+        wl_codes, wl_planes = [], []
+
+        def load_wl():
+            raw = big.tile([P, PACK, N], F32, tag="big", name="wl_raw")
+            rows = wl.rearrange("(q t s) n -> t q s n", t=PACK, s=8)
+            for t in range(PACK):
+                nc.sync.dma_start(raw[:, t, :], rows[t])
+            with nc.allow_non_contiguous_dma(reason="one gain for each partition and row tile"):
+                for t in range(PACK):
+                    nc.sync.dma_start(gain_col[t][:], gain.rearrange("(q t s) -> t q s", t=PACK, s=8)[t])
+            for t in range(PACK):
+                nc.scalar.copy(gain_rows[:, t, :], gain_col[t][:].to_broadcast([P, P3]))
+            return raw
+
+        def quantise_wl(raw, g):
+            rounded = keep.tile([P, PACK, P, PACK], BF16, align_bytes=64, name=f"wl_bf{g}")
+            nc.scalar.copy(
+                rounded[:].rearrange("p u m j -> p m j u"),
+                raw[:, :, g * 512:(g + 1) * 512].rearrange("p j (m u) -> p m j u", u=PACK),
+            )
+            codes = keep.tile([P, PACK * P], U32, align_bytes=64, name=f"wl_codes{g}")
+            plane = keep.tile([P, PACK * P], U8, align_bytes=64, name=f"wl_plane{g}")
+            nc.vector.quantize_mx(
+                out=codes[:].bitcast(FP8X4), scales=plane[:],
+                in_=rounded[:].rearrange("p u m j -> p (u m j)"),
+            )
+            wl_codes.append(codes)
+            wl_planes.append(plane)
+
+        reduce_phase(0)
+        quantise_wt(0)
+        h = features(0)
+        wl_raw = load_wl()
+        reduce_phase(1)
+        for t in range(PACK):
+            if t + 1 < PACK:
+                quantise_wt(t + 1)
+            if t + 2 < PACK:
+                reduce_phase(t + 2)
+            else:
+                quantise_wl(wl_raw, t + 2 - PACK)
+            levels(t, h)
+            if t + 1 < PACK:
+                h = features(t + 1)
+
+        a3_bf = keep.tile([P, P3, PACK], BF16, align_bytes=64)
+        nc.vector.tensor_copy(a3_bf[:], a3[:].rearrange("p t j -> p j t"))
+        a3_codes = keep.tile([P, P3], U32, align_bytes=64)
+        a3_plane = keep.tile([P, P3], U8, align_bytes=64)
+        nc.vector.quantize_mx(
+            out=a3_codes[:].bitcast(FP8X4), scales=a3_plane[:], in_=a3_bf[:].rearrange("p j t -> p (j t)"),
+        )
+
+        y_codes = keep.tile([P, GROUPS, P3], U32, align_bytes=64)
+        y_plane = keep.tile([P, GROUPS, P3], U8, align_bytes=64)
+        for g in range(GROUPS):
+            y = keep.tile([P, PACK, P3], F32, name=f"y{g}")
+            for b in range(2):
+                bank = psum.tile([P, BANK], F32, tag="bank", name="bank")
+                for i in range(2):
+                    u = 2 * b + i
+                    nc.tensor.matmul_mx(
+                        out=bank[:, i * P3:(i + 1) * P3],
+                        lhsT=wl_codes[g][:, u * P:(u + 1) * P].bitcast(FP8X4),
+                        lhsT_scale=wl_planes[g][:, u * P:(u + 1) * P],
+                        rhs=a3_codes[:].bitcast(FP8X4), rhs_scale=a3_plane[:],
+                        start=True, stop=True,
+                    )
+                rows = y[:, 2 * b:2 * b + 2, :].rearrange("p i m -> p (i m)")
+                if g == 0 and b == 1:
+                    nc.vector.tensor_copy(rows, bank[:])
+                else:
+                    nc.scalar.copy(rows, bank[:])
+            nc.sync.dma_start(out_0[g * 512:(g + 1) * 512, :].rearrange("(p u) m -> p u m", u=PACK), y[:])
+            y_bf = keep.tile([P, P3, PACK], BF16, align_bytes=64, name=f"y_bf{g}")
+            nc.vector.tensor_copy(y_bf[:], y[:].rearrange("p u m -> p m u"))
+            nc.vector.quantize_mx(
+                out=y_codes[:, g, :].bitcast(FP8X4), scales=y_plane[:, g, :],
+                in_=y_bf[:].rearrange("p m u -> p (m u)"),
+            )
+            nc.sync.dma_start(
+                out_1[g].rearrange("p m i -> p (m i)").bitcast(I32), y_codes[:, g, :].bitcast(I32),
+            )
+        for q in range(4):
+            queue = nc.sync if q % 2 == 0 else nc.scalar
+            queue.dma_start(
+                out_2[:, 4 * q:4 * q + 4, :].bitcast(I32).rearrange("g r w -> r g w"),
+                y_plane[32 * q:32 * q + 4].bitcast(I32),
+            )

@@ -169,27 +169,40 @@ def tile_list_blind_audition_heats_kernel(
                     nc.scalar.activation(tanh_tone[:, i * BANK:(i + 1) * BANK], bank[:], ACT.Tanh, bias=zero_bias[:])
                 angle = angles[t, c]
                 nc.scalar.activation(angle[:], angle[:], ACT.Sin, bias=math.pi / 2)
-                nc.vector.tensor_tensor(h[:, c * CHUNK:(c + 1) * CHUNK], tanh_tone[:], angle[:], ALU.mult)
+                for i in range(CHUNK // BANK):
+                    cols = slice(i * BANK, (i + 1) * BANK)
+                    nc.gpsimd.tensor_tensor(
+                        h[:, c * CHUNK + i * BANK:c * CHUNK + (i + 1) * BANK], tanh_tone[:, cols], angle[:, cols], ALU.mult,
+                    )
             return h
 
         gain_col = [keep.tile([P, 1], F32, name=f"gain_col{t}") for t in range(PACK)]
         gain_rows = keep.tile([P, PACK, P3], F32)
         a3 = keep.tile([P, PACK, P3], F32)
 
+        def halves(n):
+            return [(slice(i * n // 2, (i + 1) * n // 2), slice(i * n // 32, (i + 1) * n // 32)) for i in range(2)]
+
         def levels(t, h):
             left = work.tile([P, P1], F32, tag="left1", name="left1", bufs=1)
             right = work.tile([P, P1], F32, tag="right1", name="right1", bufs=1)
             a1 = work.tile([P, P1], F32, tag="a1", name="a1", bufs=1)
-            nc.vector.tensor_copy(left[:], h[:].indirect(pos[0][:]))
-            nc.vector.tensor_copy(right[:], h[:].indirect(pos[1][:]))
-            nc.vector.tensor_tensor(a1[:], left[:], right[:], ALU.max)
+            for cols, lst in halves(P1):
+                nc.vector.tensor_copy(left[:, cols], h[:].indirect(pos[0][:, lst]))
+                nc.vector.tensor_copy(right[:, cols], h[:].indirect(pos[1][:, lst]))
+            for cols, lst in halves(P1):
+                nc.vector.tensor_tensor(a1[:, cols], left[:, cols], right[:, cols], ALU.max)
             right2 = work.tile([P, P2], F32, tag="right2", name="right2", bufs=1)
             a2 = work.tile([P, P2], F32, tag="a2", name="a2", bufs=1)
-            nc.vector.tensor_copy(right2[:], a1[:].indirect(pos[3][:]))
-            nc.vector.tensor_tensor(a2[:], a1[:].indirect(pos[2][:]), right2[:], ALU.subtract)
+            for cols, lst in halves(P2):
+                nc.vector.tensor_copy(right2[:, cols], a1[:].indirect(pos[3][:, lst]))
+            for cols, lst in halves(P2):
+                nc.vector.tensor_tensor(a2[:, cols], a1[:].indirect(pos[2][:, lst]), right2[:, cols], ALU.subtract)
             left3 = work.tile([P, P3], F32, tag="left3", name="left3", bufs=1)
-            nc.vector.tensor_tensor(left3[:], a2[:].indirect(pos[4][:]), gain_rows[:, t, :], ALU.mult)
-            nc.vector.tensor_tensor(a3[:, t, :], a2[:].indirect(pos[5][:]), left3[:], ALU.mult)
+            for cols, lst in halves(P3):
+                nc.vector.tensor_tensor(left3[:, cols], a2[:].indirect(pos[4][:, lst]), gain_rows[:, t, cols], ALU.mult)
+            for cols, lst in halves(P3):
+                nc.vector.tensor_tensor(a3[:, t, cols], a2[:].indirect(pos[5][:, lst]), left3[:, cols], ALU.mult)
 
         wl_codes, wl_planes = [], []
 

@@ -2,6 +2,7 @@ import math
 from contextlib import ExitStack
 
 import concourse.mybir as mybir
+from concourse.masks import make_identity
 
 T, S, K, H, P1, P2, P3, N = 4096, 2048, 1024, 512, 1024, 512, 256, 1024
 FLOPS = 2 * (2 * K * H * S + H * N * P3)
@@ -19,11 +20,15 @@ ACT = mybir.ActivationFunctionType
 
 P = 128
 PACK = 4
-PASSES = K // (P * PACK)
+K_PASS = P * PACK
+PASSES = K // K_PASS
 BANK = 512
 CHUNK = 1024
-GROUPS = N // (P * PACK)
+CHUNKS = S // CHUNK
+GROUPS = N // K_PASS
 TWO_PI = 2.0 * math.pi
+MX_BANKS = 3
+SUM_BANKS = 3
 
 
 def tile_list_blind_audition_heats_kernel(
@@ -33,9 +38,11 @@ def tile_list_blind_audition_heats_kernel(
     nc = tc.nc
     with ExitStack() as ctx:
         keep = ctx.enter_context(tc.tile_pool(name="keep", bufs=1))
-        big = ctx.enter_context(tc.tile_pool(name="big", bufs=2))
-        work = ctx.enter_context(tc.tile_pool(name="work", bufs=2))
-        psum = ctx.enter_context(tc.psum_pool(name="psum", bufs=8))
+        shared = ctx.enter_context(tc.tile_pool(name="shared", bufs=1))
+        psum = ctx.enter_context(tc.psum_pool(name="psum", bufs=1))
+
+        def tiles(name, count, shape, dtype):
+            return [keep.tile(shape, dtype, align_bytes=64, name=f"{name}{i}") for i in range(count)]
 
         def load_list(name, src):
             tile = keep.tile(list(src.shape), U16, name=name)
@@ -51,11 +58,16 @@ def tile_list_blind_audition_heats_kernel(
         )
         nc.vector.memset(scale_win[0:96, :].bitcast(I32), 0)
 
-        word_win = []
-        for a in range(PASSES):
-            win = big.tile([P, T], I32, tag="big", name=f"word_win{a}")
-            nc.sync.dma_start(win[:], tab_words[a].rearrange("p t i -> p (t i)").bitcast(I32))
-            word_win.append(win)
+        word_win = [shared.tile([P, T], I32, name=f"word_win{a}", offset=a * 4 * T) for a in range(PASSES)]
+        wc_raw = keep.tile([P, PASSES, 2 * H], U8)
+        wt_raw = tiles("wt_raw", PASSES, [P, PACK, H], F32)
+
+        def load_words(a):
+            nc.sync.dma_start(word_win[a][:], tab_words[a].rearrange("p t i -> p (t i)").bitcast(I32))
+
+        load_words(0)
+        nc.sync.dma_start(wc_raw[:].bitcast(I32), wc_words.bitcast(I32).rearrange("a p w -> p a w"))
+        load_words(1)
 
         zero_in = keep.tile([P, 1], F32)
         zero_bias = keep.tile([P, 1], F32)
@@ -70,68 +82,90 @@ def tile_list_blind_audition_heats_kernel(
                 wc_scales[:, 4 * q:4 * q + 4, :].bitcast(I32).rearrange("a r w -> r a w"),
             )
 
-        wc_raw = keep.tile([P, PASSES, 2 * H], U8)
-        nc.sync.dma_start(wc_raw[:].bitcast(I32), wc_words.bitcast(I32).rearrange("a p w -> p a w"))
-
-        wt_raw = []
-        for a in range(PASSES):
-            raw = keep.tile([P, PACK, H], F32, name=f"wt_raw{a}")
-            nc.sync.dma_start(raw[:], wt[a * 512:(a + 1) * 512, :].rearrange("(p j) c -> p j c", j=PACK))
-            wt_raw.append(raw)
-
-        pos = [load_list("pos_sb0", pos1)]
-
         v_scales = keep.tile([P, PASSES * S], U8, align_bytes=64)
         nc.gpsimd.memset(v_scales[:].bitcast(I32), 0)
         picked_scales = keep.tile([P, S], U8)
         nc.vector.tensor_copy(picked_scales[:], scale_win[:].indirect(offs_sb[:]))
-        for q in range(4):
+
+        def place_scales(q):
             nc.scalar.dma_start(
                 v_scales[32 * q:32 * q + 4, :].bitcast(I32),
                 picked_scales[96 + 8 * q:96 + 8 * q + 8, :].bitcast(I32),
             )
+
+        place_scales(0)
+        for a in range(PASSES):
+            nc.sync.dma_start(
+                wt_raw[a][:], wt[a * K_PASS:(a + 1) * K_PASS, :].rearrange("(p j) c -> p j c", j=PACK),
+            )
+        pos = [load_list("pos_sb0", pos1)]
+        for q in range(1, 4):
+            place_scales(q)
         pos.extend(load_list(f"pos_sb{i + 1}", src) for i, src in enumerate((pos2, pos3, pos4, pos5, pos6)))
 
-        v_words = [keep.tile([P, S], U32, align_bytes=64, name=f"v_words{a}") for a in range(PASSES)]
+        ident = keep.tile([P, P], F32)
+        make_identity(nc, ident[:])
+
+        v_words = tiles("v_words", PASSES, [P, S], U32)
         nc.vector.tensor_copy(v_words[0][:], word_win[0][:].bitcast(U32).indirect(offs_sb[:]))
 
-        wc_codes = keep.tile([P, PASSES, PACK, 2 * P], U8, align_bytes=64)
-        wc_planes = keep.tile([P, PASSES, PACK, P], U8, align_bytes=64)
+        wc_codes = shared.tile([P, PASSES, PACK, 2 * P], U8, align_bytes=64, offset=0)
+        wc_planes = shared.tile([P, PASSES, PACK, P], U8, align_bytes=64, offset=2048)
         nc.vector.tensor_copy(
             wc_planes[:].bitcast(I32).rearrange("p a t (q w) -> p a t q w", w=2),
             wcs_raw[:].bitcast(I32).rearrange("p a (q t w) -> p a t q w", t=PACK, w=2),
+        )
+        nc.vector.tensor_copy(
+            wc_codes[:].bitcast(I32).rearrange("p a t (q w) -> p a t q w", w=4),
+            wc_raw[:].bitcast(I32).rearrange("p a (q t w) -> p a t q w", t=PACK, w=4),
         )
         for s in range(S // BANK):
             nc.vector.tensor_copy(
                 v_words[1][:, s * BANK:(s + 1) * BANK],
                 word_win[1][:].bitcast(U32).indirect(offs_sb[:, s * BANK // 16:(s + 1) * BANK // 16]),
             )
-            if s == 0:
-                nc.vector.tensor_copy(
-                    wc_codes[:].bitcast(I32).rearrange("p a t (q w) -> p a t q w", w=4),
-                    wc_raw[:].bitcast(I32).rearrange("p a (q t w) -> p a t q w", t=PACK, w=4),
-                )
 
-        wt_codes, wt_planes = [], []
+        wl_raw = shared.tile([P, PACK, N], F32, offset=4096)
+        wl_rows = wl.rearrange("(q t s) n -> t q s n", t=PACK, s=8)
+        for t in range(PACK):
+            nc.sync.dma_start(wl_raw[:, t, :], wl_rows[t])
+        gain_col = [shared.tile([P, 1], F32, name=f"gain_col{t}", offset=24576 + 64 * t) for t in range(PACK)]
+        with nc.allow_non_contiguous_dma(reason="one gain for each partition and row tile"):
+            for t in range(PACK):
+                nc.sync.dma_start(gain_col[t][:], gain.rearrange("(q t s) -> t q s", t=PACK, s=8)[t])
+
+        wt_bf = [
+            shared.tile([P, PASSES, P, PACK], BF16, align_bytes=64, name=f"wt_bf{i}", offset=20480 + 2048 * i)
+            for i in range(2)
+        ]
+        wt_codes = tiles("wt_codes", PACK, [P, PASSES * P], U32)
+        wt_planes = tiles("wt_plane", PACK, [P, PASSES * P], U8)
 
         def quantise_wt(t):
-            rounded = keep.tile([P, PASSES, P, PACK], BF16, align_bytes=64, name=f"wt_bf{t}")
+            rounded = wt_bf[t % 2]
             for a in range(PASSES):
-                nc.scalar.copy(
+                nc.vector.tensor_copy(
                     rounded[:, a].rearrange("p (q s) j -> p q s j", s=8),
                     wt_raw[a][:].rearrange("p j (q t s) -> p t q s j", t=PACK, s=8)[:, t],
                 )
-            codes = keep.tile([P, PASSES * P], U32, align_bytes=64, name=f"wt_codes{t}")
-            plane = keep.tile([P, PASSES * P], U8, align_bytes=64, name=f"wt_plane{t}")
             nc.vector.quantize_mx(
-                out=codes[:].bitcast(FP8X4), scales=plane[:],
+                out=wt_codes[t][:].bitcast(FP8X4), scales=wt_planes[t][:],
                 in_=rounded[:].rearrange("p a m j -> p (a m j)"),
             )
-            wt_codes.append(codes)
-            wt_planes.append(plane)
 
-        def product(codes, planes, s):
-            bank = psum.tile([P, BANK], F32, tag="bank", name="bank")
+        banks = [psum.tile([P, BANK], F32, name=f"bank{b}") for b in range(8)]
+        mx_turn, sum_turn = [], []
+
+        def next_mx_bank():
+            mx_turn.append(0)
+            return banks[len(mx_turn) % MX_BANKS]
+
+        def next_sum_bank():
+            sum_turn.append(0)
+            return banks[MX_BANKS + len(sum_turn) % SUM_BANKS]
+
+        def weights_times_v(codes, planes, s):
+            bank = next_mx_bank()
             for a in range(PASSES):
                 nc.tensor.matmul_mx(
                     out=bank[:], lhsT=codes[a], lhsT_scale=planes[a],
@@ -141,149 +175,184 @@ def tile_list_blind_audition_heats_kernel(
                 )
             return bank
 
-        angles = {}
+        def v_times_wc(t, s):
+            bank = next_mx_bank()
+            for b in range(BANK // P):
+                first = s * BANK + b * P
+                for a in range(PASSES):
+                    nc.tensor.matmul_mx(
+                        out=bank[:, b * P:(b + 1) * P],
+                        lhsT=v_words[a][:, first:first + P].bitcast(FP8X4),
+                        lhsT_scale=v_scales[:, a * S + first:a * S + first + P],
+                        rhs=wc_codes[:, a, t, :].bitcast(FP4X4), rhs_scale=wc_planes[:, a, t, :],
+                        start=(a == 0), stop=(a == PASSES - 1),
+                    )
+            return bank
 
-        def reduce_phase(t):
-            codes = [wc_codes[:, a, t, :].bitcast(FP4X4) for a in range(PASSES)]
-            planes = [wc_planes[:, a, t, :] for a in range(PASSES)]
-            for c in range(S // CHUNK):
-                angle = work.tile([P, CHUNK], F32, tag="angle", name="angle", bufs=6)
-                turns = work.tile([P, CHUNK], U32, tag="turns", name="turns", bufs=4)
-                for i in range(CHUNK // BANK):
-                    bank = product(codes, planes, c * CHUNK // BANK + i)
-                    nc.scalar.activation(angle[:, i * BANK:(i + 1) * BANK], bank[:], ACT.Abs)
-                nc.scalar.activation(turns[:], angle[:], ACT.Copy, scale=1.0 / TWO_PI, bias=-0.25)
-                nc.vector.scalar_tensor_tensor(
-                    angle[:], turns[:].bitcast(I32), TWO_PI, angle[:], ALU.mult, ALU.subtract,
-                )
-                angles[t, c] = angle
+        cos_buf = tiles("cos_buf", 2 * CHUNKS, [P, CHUNK], F32)
+        tanh_buf = tiles("tanh_buf", 2 * CHUNKS, [P, CHUNK], F32)
+        angle_buf = tiles("angle_buf", CHUNKS, [P, CHUNK], F32)
+        turns_buf = tiles("turns_buf", CHUNKS, [P, CHUNK], I32)
+        back_buf = tiles("back_buf", CHUNKS, [P, CHUNK], F32)
+        h_buf = tiles("h_buf", 2, [P, S], F32)
 
-        def features(t):
-            h = work.tile([P, S], F32, tag="h", name="h")
+        def slices(c):
+            return [(c * CHUNK // BANK + i, slice(i * BANK, (i + 1) * BANK)) for i in range(CHUNK // BANK)]
+
+        def tanh_tone(t, c):
             codes = [wt_codes[t][:, a * P:(a + 1) * P].bitcast(FP8X4) for a in range(PASSES)]
             planes = [wt_planes[t][:, a * P:(a + 1) * P] for a in range(PASSES)]
-            for c in range(S // CHUNK):
-                tanh_tone = work.tile([P, CHUNK], F32, tag="tanh_tone", name="tanh_tone", bufs=4)
-                for i in range(CHUNK // BANK):
-                    bank = product(codes, planes, c * CHUNK // BANK + i)
-                    nc.scalar.activation(tanh_tone[:, i * BANK:(i + 1) * BANK], bank[:], ACT.Tanh, bias=zero_bias[:])
-                angle = angles[t, c]
-                nc.scalar.activation(angle[:], angle[:], ACT.Sin, bias=math.pi / 2)
-                for i in range(CHUNK // BANK):
-                    cols = slice(i * BANK, (i + 1) * BANK)
-                    nc.gpsimd.tensor_tensor(
-                        h[:, c * CHUNK + i * BANK:c * CHUNK + (i + 1) * BANK], tanh_tone[:, cols], angle[:, cols], ALU.mult,
-                    )
-            return h
+            for s, cols in slices(c):
+                bank = weights_times_v(codes, planes, s)
+                nc.scalar.activation(
+                    tanh_buf[(t % 2) * CHUNKS + c][:, cols], bank[:], ACT.Tanh, bias=zero_bias[:],
+                )
 
-        gain_col = [keep.tile([P, 1], F32, name=f"gain_col{t}") for t in range(PACK)]
+        def multiply(t, c):
+            i = (t % 2) * CHUNKS + c
+            nc.vector.tensor_tensor(
+                h_buf[t % 2][:, c * CHUNK:(c + 1) * CHUNK], tanh_buf[i][:], cos_buf[i][:], ALU.mult,
+            )
+
+        def features_first():
+            wc_c = [wc_codes[:, a, 0, :].bitcast(FP4X4) for a in range(PASSES)]
+            wc_p = [wc_planes[:, a, 0, :] for a in range(PASSES)]
+            wt_c = [wt_codes[0][:, a * P:(a + 1) * P].bitcast(FP8X4) for a in range(PASSES)]
+            wt_p = [wt_planes[0][:, a * P:(a + 1) * P] for a in range(PASSES)]
+            for c in range(CHUNKS):
+                for s, cols in slices(c):
+                    bank = weights_times_v(wc_c, wc_p, s)
+                    nc.scalar.activation(angle_buf[c][:, cols], bank[:], ACT.Abs)
+                    nc.vector.tensor_scalar(
+                        turns_buf[c][:, cols], angle_buf[c][:, cols], 1.0 / TWO_PI, -0.25, ALU.mult, ALU.add,
+                    )
+                    nc.vector.scalar_tensor_tensor(
+                        angle_buf[c][:, cols], turns_buf[c][:, cols], -TWO_PI, angle_buf[c][:, cols], ALU.mult, ALU.add,
+                    )
+            for c in range(CHUNKS):
+                for s, cols in slices(c):
+                    bank = weights_times_v(wt_c, wt_p, s)
+                    nc.scalar.activation(tanh_buf[c][:, cols], bank[:], ACT.Tanh, bias=zero_bias[:])
+                    nc.scalar.activation(
+                        cos_buf[c][:, cols], angle_buf[c][:, cols], ACT.Sin, scale=-1.0, bias=math.pi / 2,
+                    )
+                    nc.vector.tensor_tensor(
+                        h_buf[0][:, s * BANK:(s + 1) * BANK], tanh_buf[c][:, cols], cos_buf[c][:, cols], ALU.mult,
+                    )
+
+        def features(t, c):
+            angle, back = angle_buf[CHUNKS - 1 - c], back_buf[c]
+            for s, cols in slices(c):
+                bank = v_times_wc(t, s)
+                nc.scalar.activation(angle[:, cols], bank[:], ACT.Abs)
+            turns = turns_buf[c][:].bitcast(U32)
+            nc.scalar.activation(turns, angle[:], ACT.Copy, scale=1.0 / TWO_PI, bias=-0.25)
+            nc.scalar.activation(back[:], turns, ACT.Copy, scale=-TWO_PI)
+            sums = []
+            for s, cols in slices(c):
+                bank = next_sum_bank()
+                for b in range(BANK // P):
+                    block = slice(cols.start + b * P, cols.start + (b + 1) * P)
+                    for part in (angle, back):
+                        nc.tensor.matmul(
+                            bank[:, b * P:(b + 1) * P], part[:, block], ident[:], is_transpose=True,
+                            start=part is angle, stop=part is back,
+                        )
+                sums.append(bank)
+            tanh_tone(t, c)
+            for (s, cols), bank in zip(slices(c), sums):
+                nc.scalar.activation(
+                    cos_buf[(t % 2) * CHUNKS + c][:, cols], bank[:], ACT.Sin, scale=-1.0, bias=math.pi / 2,
+                )
+            multiply(t, c)
+
         gain_rows = keep.tile([P, PACK, P3], F32)
         a3 = keep.tile([P, PACK, P3], F32)
+        left1 = keep.tile([P, P1], F32)
+        right1 = keep.tile([P, P1], F32)
+        a1 = keep.tile([P, P1], F32)
+        right2 = keep.tile([P, P2], F32)
+        a2 = keep.tile([P, P2], F32)
+        left3 = keep.tile([P, P3], F32)
 
         def halves(n):
             return [(slice(i * n // 2, (i + 1) * n // 2), slice(i * n // 32, (i + 1) * n // 32)) for i in range(2)]
 
-        def levels(t, h):
-            left = work.tile([P, P1], F32, tag="left1", name="left1", bufs=1)
-            right = work.tile([P, P1], F32, tag="right1", name="right1", bufs=1)
-            a1 = work.tile([P, P1], F32, tag="a1", name="a1", bufs=1)
+        def levels(t):
+            h = h_buf[t % 2]
+            nc.scalar.copy(gain_rows[:, t, :], gain_col[t][:].to_broadcast([P, P3]))
             for cols, lst in halves(P1):
-                nc.vector.tensor_copy(left[:, cols], h[:].indirect(pos[0][:, lst]))
-                nc.vector.tensor_copy(right[:, cols], h[:].indirect(pos[1][:, lst]))
+                nc.vector.tensor_copy(left1[:, cols], h[:].indirect(pos[0][:, lst]))
+                nc.vector.tensor_copy(right1[:, cols], h[:].indirect(pos[1][:, lst]))
             for cols, lst in halves(P1):
-                nc.vector.tensor_tensor(a1[:, cols], left[:, cols], right[:, cols], ALU.max)
-            right2 = work.tile([P, P2], F32, tag="right2", name="right2", bufs=1)
-            a2 = work.tile([P, P2], F32, tag="a2", name="a2", bufs=1)
+                nc.vector.tensor_tensor(a1[:, cols], left1[:, cols], right1[:, cols], ALU.max)
             for cols, lst in halves(P2):
                 nc.vector.tensor_copy(right2[:, cols], a1[:].indirect(pos[3][:, lst]))
             for cols, lst in halves(P2):
                 nc.vector.tensor_tensor(a2[:, cols], a1[:].indirect(pos[2][:, lst]), right2[:, cols], ALU.subtract)
-            left3 = work.tile([P, P3], F32, tag="left3", name="left3", bufs=1)
             for cols, lst in halves(P3):
                 nc.vector.tensor_tensor(left3[:, cols], a2[:].indirect(pos[4][:, lst]), gain_rows[:, t, cols], ALU.mult)
             for cols, lst in halves(P3):
                 nc.vector.tensor_tensor(a3[:, t, cols], a2[:].indirect(pos[5][:, lst]), left3[:, cols], ALU.mult)
 
-        wl_codes, wl_planes = [], []
+        wl_codes = tiles("wl_codes", GROUPS, [P, PACK * P], U32)
+        wl_planes = tiles("wl_plane", GROUPS, [P, PACK * P], U8)
 
-        def load_wl():
-            raw = big.tile([P, PACK, N], F32, tag="big", name="wl_raw")
-            rows = wl.rearrange("(q t s) n -> t q s n", t=PACK, s=8)
-            for t in range(PACK):
-                nc.sync.dma_start(raw[:, t, :], rows[t])
-            with nc.allow_non_contiguous_dma(reason="one gain for each partition and row tile"):
-                for t in range(PACK):
-                    nc.sync.dma_start(gain_col[t][:], gain.rearrange("(q t s) -> t q s", t=PACK, s=8)[t])
-            for t in range(PACK):
-                nc.scalar.copy(gain_rows[:, t, :], gain_col[t][:].to_broadcast([P, P3]))
-            return raw
-
-        def quantise_wl(raw, g):
-            rounded = keep.tile([P, PACK, P, PACK], BF16, align_bytes=64, name=f"wl_bf{g}")
+        def quantise_wl(g):
+            rounded = tanh_buf[CHUNKS + g][:].bitcast(BF16)
             nc.scalar.copy(
-                rounded[:].rearrange("p u m j -> p m j u"),
-                raw[:, :, g * 512:(g + 1) * 512].rearrange("p j (m u) -> p m j u", u=PACK),
+                rounded.rearrange("p (u m j) -> p m j u", u=PACK, j=PACK),
+                wl_raw[:, :, g * K_PASS:(g + 1) * K_PASS].rearrange("p j (m u) -> p m j u", u=PACK),
             )
-            codes = keep.tile([P, PACK * P], U32, align_bytes=64, name=f"wl_codes{g}")
-            plane = keep.tile([P, PACK * P], U8, align_bytes=64, name=f"wl_plane{g}")
-            nc.vector.quantize_mx(
-                out=codes[:].bitcast(FP8X4), scales=plane[:],
-                in_=rounded[:].rearrange("p u m j -> p (u m j)"),
-            )
-            wl_codes.append(codes)
-            wl_planes.append(plane)
+            nc.vector.quantize_mx(out=wl_codes[g][:].bitcast(FP8X4), scales=wl_planes[g][:], in_=rounded)
 
-        reduce_phase(0)
         quantise_wt(0)
-        h = features(0)
-        wl_raw = load_wl()
-        reduce_phase(1)
+        features_first()
+        for t in range(1, PACK):
+            quantise_wt(t)
         for t in range(PACK):
-            if t + 1 < PACK:
-                quantise_wt(t + 1)
-            if t + 2 < PACK:
-                reduce_phase(t + 2)
-            else:
-                quantise_wl(wl_raw, t + 2 - PACK)
-            levels(t, h)
-            if t + 1 < PACK:
-                h = features(t + 1)
+            levels(t)
+            for c in range(CHUNKS):
+                if t + 1 < PACK:
+                    features(t + 1, c)
+                else:
+                    quantise_wl(c)
 
         a3_bf = keep.tile([P, P3, PACK], BF16, align_bytes=64)
-        nc.vector.tensor_copy(a3_bf[:], a3[:].rearrange("p t j -> p j t"))
         a3_codes = keep.tile([P, P3], U32, align_bytes=64)
         a3_plane = keep.tile([P, P3], U8, align_bytes=64)
-        nc.vector.quantize_mx(
-            out=a3_codes[:].bitcast(FP8X4), scales=a3_plane[:], in_=a3_bf[:].rearrange("p j t -> p (j t)"),
-        )
+        for cols, lst in halves(P3):
+            nc.vector.tensor_copy(a3_bf[:, cols, :], a3[:, :, cols].rearrange("p t j -> p j t"))
+        for cols, lst in halves(P3):
+            nc.vector.quantize_mx(
+                out=a3_codes[:, cols].bitcast(FP8X4), scales=a3_plane[:, cols],
+                in_=a3_bf[:, cols, :].rearrange("p j t -> p (j t)"),
+            )
 
+        y = tiles("y", GROUPS, [P, PACK, P3], F32)
+        y_bf = tiles("y_bf", GROUPS, [P, P3, PACK], BF16)
         y_codes = keep.tile([P, GROUPS, P3], U32, align_bytes=64)
         y_plane = keep.tile([P, GROUPS, P3], U8, align_bytes=64)
-        for g in range(GROUPS):
-            y = keep.tile([P, PACK, P3], F32, name=f"y{g}")
-            for b in range(2):
-                bank = psum.tile([P, BANK], F32, tag="bank", name="bank")
-                for i in range(2):
-                    u = 2 * b + i
+        for i, (cols, lst) in enumerate(halves(P3)):
+            for g in range(GROUPS):
+                bank = banks[i * GROUPS + g]
+                for u in range(PACK):
                     nc.tensor.matmul_mx(
-                        out=bank[:, i * P3:(i + 1) * P3],
+                        out=bank[:, u * P:(u + 1) * P],
                         lhsT=wl_codes[g][:, u * P:(u + 1) * P].bitcast(FP8X4),
                         lhsT_scale=wl_planes[g][:, u * P:(u + 1) * P],
-                        rhs=a3_codes[:].bitcast(FP8X4), rhs_scale=a3_plane[:],
+                        rhs=a3_codes[:, cols].bitcast(FP8X4), rhs_scale=a3_plane[:, cols],
                         start=True, stop=True,
                     )
-                rows = y[:, 2 * b:2 * b + 2, :].rearrange("p i m -> p (i m)")
-                if g == 0 and b == 1:
-                    nc.vector.tensor_copy(rows, bank[:])
-                else:
-                    nc.scalar.copy(rows, bank[:])
-            nc.sync.dma_start(out_0[g * 512:(g + 1) * 512, :].rearrange("(p u) m -> p u m", u=PACK), y[:])
-            y_bf = keep.tile([P, P3, PACK], BF16, align_bytes=64, name=f"y_bf{g}")
-            nc.vector.tensor_copy(y_bf[:], y[:].rearrange("p u m -> p m u"))
-            nc.vector.quantize_mx(
-                out=y_codes[:, g, :].bitcast(FP8X4), scales=y_plane[:, g, :],
-                in_=y_bf[:].rearrange("p m u -> p (m u)"),
-            )
+                nc.scalar.copy(y[g][:, :, cols], bank[:].rearrange("p (u m) -> p u m", u=PACK))
+                nc.vector.tensor_copy(y_bf[g][:, cols, :], y[g][:, :, cols].rearrange("p u m -> p m u"))
+                nc.vector.quantize_mx(
+                    out=y_codes[:, g, cols].bitcast(FP8X4), scales=y_plane[:, g, cols],
+                    in_=y_bf[g][:, cols, :].rearrange("p m u -> p (m u)"),
+                )
+        for g in range(GROUPS):
+            nc.sync.dma_start(out_0[g * K_PASS:(g + 1) * K_PASS, :].rearrange("(p u) m -> p u m", u=PACK), y[g][:])
+        for g in range(GROUPS):
             nc.sync.dma_start(
                 out_1[g].rearrange("p m i -> p (m i)").bitcast(I32), y_codes[:, g, :].bitcast(I32),
             )

@@ -27,8 +27,8 @@ CHUNK = 1024
 CHUNKS = S // CHUNK
 GROUPS = N // K_PASS
 TWO_PI = 2.0 * math.pi
-MX_BANKS = 3
-SUM_BANKS = 3
+MX_BANKS = 4
+SUM_BANKS = 4
 
 
 def tile_list_blind_audition_heats_kernel(
@@ -51,7 +51,7 @@ def tile_list_blind_audition_heats_kernel(
 
         offs_sb = load_list("offs_sb", offs)
 
-        scale_win = keep.tile([P, T], U8)
+        scale_win = shared.tile([P, T], U8, offset=32768)
         nc.sync.dma_start(
             scale_win[96:P, :].bitcast(I32),
             tab_scales.bitcast(I32).rearrange("a q w -> q a w"),
@@ -60,7 +60,7 @@ def tile_list_blind_audition_heats_kernel(
 
         word_win = [shared.tile([P, T], I32, name=f"word_win{a}", offset=a * 4 * T) for a in range(PASSES)]
         wc_raw = keep.tile([P, PASSES, 2 * H], U8)
-        wt_raw = tiles("wt_raw", PASSES, [P, PACK, H], F32)
+        wt_raw = [shared.tile([P, PACK, H], F32, name=f"wt_raw{a}", offset=36864 + 8192 * a) for a in range(PASSES)]
 
         def load_words(a):
             nc.sync.dma_start(word_win[a][:], tab_words[a].rearrange("p t i -> p (t i)").bitcast(I32))
@@ -74,7 +74,7 @@ def tile_list_blind_audition_heats_kernel(
         nc.gpsimd.memset(zero_in[:], 0.0)
         nc.scalar.activation(zero_bias[:], zero_in[:], ACT.Silu)
 
-        wcs_raw = keep.tile([P, PASSES, H], U8)
+        wcs_raw = shared.tile([P, PASSES, H], U8, offset=36864)
         nc.gpsimd.memset(wcs_raw[:].bitcast(I32), 0)
         for q in range(4):
             nc.scalar.dma_start(
@@ -86,6 +86,12 @@ def tile_list_blind_audition_heats_kernel(
         nc.gpsimd.memset(v_scales[:].bitcast(I32), 0)
         picked_scales = keep.tile([P, S], U8)
         nc.vector.tensor_copy(picked_scales[:], scale_win[:].indirect(offs_sb[:]))
+
+        wc_planes = shared.tile([P, PASSES, PACK, P], U8, align_bytes=64, offset=32768)
+        nc.vector.tensor_copy(
+            wc_planes[:].bitcast(I32).rearrange("p a t (q w) -> p a t q w", w=2),
+            wcs_raw[:].bitcast(I32).rearrange("p a (q t w) -> p a t q w", t=PACK, w=2),
+        )
 
         def place_scales(q):
             nc.scalar.dma_start(
@@ -109,13 +115,8 @@ def tile_list_blind_audition_heats_kernel(
         v_words = tiles("v_words", PASSES, [P, S], U32)
         nc.vector.tensor_copy(v_words[0][:], word_win[0][:].bitcast(U32).indirect(offs_sb[:]))
 
-        wc_codes = shared.tile([P, PASSES, PACK, 2 * P], U8, align_bytes=64, offset=0)
-        wc_planes = shared.tile([P, PASSES, PACK, P], U8, align_bytes=64, offset=2048)
-        nc.vector.tensor_copy(
-            wc_planes[:].bitcast(I32).rearrange("p a t (q w) -> p a t q w", w=2),
-            wcs_raw[:].bitcast(I32).rearrange("p a (q t w) -> p a t q w", t=PACK, w=2),
-        )
-        nc.vector.tensor_copy(
+        wc_codes = keep.tile([P, PASSES, PACK, 2 * P], U8, align_bytes=64)
+        nc.gpsimd.tensor_copy(
             wc_codes[:].bitcast(I32).rearrange("p a t (q w) -> p a t q w", w=4),
             wc_raw[:].bitcast(I32).rearrange("p a (q t w) -> p a t q w", t=PACK, w=4),
         )
@@ -129,20 +130,18 @@ def tile_list_blind_audition_heats_kernel(
         wl_rows = wl.rearrange("(q t s) n -> t q s n", t=PACK, s=8)
         for t in range(PACK):
             nc.sync.dma_start(wl_raw[:, t, :], wl_rows[t])
-        gain_col = [shared.tile([P, 1], F32, name=f"gain_col{t}", offset=24576 + 64 * t) for t in range(PACK)]
+        gain_col = tiles("gain_col", PACK, [P, 1], F32)
         with nc.allow_non_contiguous_dma(reason="one gain for each partition and row tile"):
             for t in range(PACK):
                 nc.sync.dma_start(gain_col[t][:], gain.rearrange("(q t s) -> t q s", t=PACK, s=8)[t])
 
-        wt_bf = [
-            shared.tile([P, PASSES, P, PACK], BF16, align_bytes=64, name=f"wt_bf{i}", offset=20480 + 2048 * i)
-            for i in range(2)
-        ]
+        wt_bf_first = shared.tile([P, PASSES, P, PACK], BF16, align_bytes=64, offset=27648)
+        wt_bf_rest = shared.tile([P, PASSES, P, PACK], BF16, align_bytes=64, offset=28672)
         wt_codes = tiles("wt_codes", PACK, [P, PASSES * P], U32)
         wt_planes = tiles("wt_plane", PACK, [P, PASSES * P], U8)
 
         def quantise_wt(t):
-            rounded = wt_bf[t % 2]
+            rounded = wt_bf_first if t == 0 else wt_bf_rest
             for a in range(PASSES):
                 nc.vector.tensor_copy(
                     rounded[:, a].rearrange("p (q s) j -> p q s j", s=8),
@@ -192,8 +191,9 @@ def tile_list_blind_audition_heats_kernel(
         cos_buf = tiles("cos_buf", 2 * CHUNKS, [P, CHUNK], F32)
         tanh_buf = tiles("tanh_buf", 2 * CHUNKS, [P, CHUNK], F32)
         angle_buf = tiles("angle_buf", CHUNKS, [P, CHUNK], F32)
-        turns_buf = tiles("turns_buf", CHUNKS, [P, CHUNK], I32)
-        back_buf = tiles("back_buf", CHUNKS, [P, CHUNK], F32)
+        turns_buf = tiles("turns_buf", CHUNKS, [P, CHUNK], U32)
+        back_all = shared.tile([P, S], F32, offset=20480)
+        back_buf = [back_all[:, c * CHUNK:(c + 1) * CHUNK] for c in range(CHUNKS)]
         h_buf = tiles("h_buf", 2, [P, S], F32)
 
         def slices(c):
@@ -223,32 +223,34 @@ def tile_list_blind_audition_heats_kernel(
                 for s, cols in slices(c):
                     bank = weights_times_v(wc_c, wc_p, s)
                     nc.scalar.activation(angle_buf[c][:, cols], bank[:], ACT.Abs)
-                    nc.vector.tensor_scalar(
-                        turns_buf[c][:, cols], angle_buf[c][:, cols], 1.0 / TWO_PI, -0.25, ALU.mult, ALU.add,
+                    nc.scalar.activation(
+                        turns_buf[c][:, cols], angle_buf[c][:, cols], ACT.Copy, scale=1.0 / TWO_PI, bias=-0.25,
                     )
                     nc.vector.scalar_tensor_tensor(
-                        angle_buf[c][:, cols], turns_buf[c][:, cols], -TWO_PI, angle_buf[c][:, cols], ALU.mult, ALU.add,
+                        back_buf[c][:, cols], turns_buf[c][:, cols].bitcast(I32), -TWO_PI, angle_buf[c][:, cols],
+                        ALU.mult, ALU.add,
                     )
             for c in range(CHUNKS):
                 for s, cols in slices(c):
                     bank = weights_times_v(wt_c, wt_p, s)
                     nc.scalar.activation(tanh_buf[c][:, cols], bank[:], ACT.Tanh, bias=zero_bias[:])
                     nc.scalar.activation(
-                        cos_buf[c][:, cols], angle_buf[c][:, cols], ACT.Sin, scale=-1.0, bias=math.pi / 2,
+                        cos_buf[c][:, cols], back_buf[c][:, cols], ACT.Sin, scale=-1.0, bias=math.pi / 2,
                     )
                     nc.vector.tensor_tensor(
                         h_buf[0][:, s * BANK:(s + 1) * BANK], tanh_buf[c][:, cols], cos_buf[c][:, cols], ALU.mult,
                     )
 
-        def features(t, c):
-            angle, back = angle_buf[CHUNKS - 1 - c], back_buf[c]
+        sums = {}
+
+        def reduce_phase(t, c):
+            angle, back = angle_buf[c], back_buf[c]
             for s, cols in slices(c):
                 bank = v_times_wc(t, s)
                 nc.scalar.activation(angle[:, cols], bank[:], ACT.Abs)
-            turns = turns_buf[c][:].bitcast(U32)
+            turns = turns_buf[c][:]
             nc.scalar.activation(turns, angle[:], ACT.Copy, scale=1.0 / TWO_PI, bias=-0.25)
-            nc.scalar.activation(back[:], turns, ACT.Copy, scale=-TWO_PI)
-            sums = []
+            nc.scalar.activation(back, turns, ACT.Copy, scale=-TWO_PI)
             for s, cols in slices(c):
                 bank = next_sum_bank()
                 for b in range(BANK // P):
@@ -258,11 +260,13 @@ def tile_list_blind_audition_heats_kernel(
                             bank[:, b * P:(b + 1) * P], part[:, block], ident[:], is_transpose=True,
                             start=part is angle, stop=part is back,
                         )
-                sums.append(bank)
+                sums[t, s] = bank
+
+        def features(t, c):
             tanh_tone(t, c)
-            for (s, cols), bank in zip(slices(c), sums):
+            for s, cols in slices(c):
                 nc.scalar.activation(
-                    cos_buf[(t % 2) * CHUNKS + c][:, cols], bank[:], ACT.Sin, scale=-1.0, bias=math.pi / 2,
+                    cos_buf[(t % 2) * CHUNKS + c][:, cols], sums[t, s][:], ACT.Sin, scale=-1.0, bias=math.pi / 2,
                 )
             multiply(t, c)
 
@@ -271,21 +275,23 @@ def tile_list_blind_audition_heats_kernel(
         left1 = keep.tile([P, P1], F32)
         right1 = keep.tile([P, P1], F32)
         a1 = keep.tile([P, P1], F32)
-        right2 = keep.tile([P, P2], F32)
         a2 = keep.tile([P, P2], F32)
-        left3 = keep.tile([P, P3], F32)
 
         def halves(n):
             return [(slice(i * n // 2, (i + 1) * n // 2), slice(i * n // 32, (i + 1) * n // 32)) for i in range(2)]
 
-        def levels(t):
+        def first_level(t):
             h = h_buf[t % 2]
-            nc.scalar.copy(gain_rows[:, t, :], gain_col[t][:].to_broadcast([P, P3]))
+            nc.gpsimd.tensor_copy(gain_rows[:, t, :], gain_col[t][:].to_broadcast([P, P3]))
             for cols, lst in halves(P1):
                 nc.vector.tensor_copy(left1[:, cols], h[:].indirect(pos[0][:, lst]))
                 nc.vector.tensor_copy(right1[:, cols], h[:].indirect(pos[1][:, lst]))
             for cols, lst in halves(P1):
                 nc.vector.tensor_tensor(a1[:, cols], left1[:, cols], right1[:, cols], ALU.max)
+
+        def later_levels(t):
+            spent = min(t + 1, PACK - 1) % 2 * CHUNKS
+            right2, left3 = (tanh_buf[spent], tanh_buf[spent + 1]) if t > 0 else (tanh_buf[0], tanh_buf[1])
             for cols, lst in halves(P2):
                 nc.vector.tensor_copy(right2[:, cols], a1[:].indirect(pos[3][:, lst]))
             for cols, lst in halves(P2):
@@ -310,13 +316,21 @@ def tile_list_blind_audition_heats_kernel(
         features_first()
         for t in range(1, PACK):
             quantise_wt(t)
-        for t in range(PACK):
-            levels(t)
-            for c in range(CHUNKS):
-                if t + 1 < PACK:
-                    features(t + 1, c)
-                else:
-                    quantise_wl(c)
+        chunks = [(t, c) for t in range(1, PACK) for c in range(CHUNKS)]
+        first_level(0)
+        later_levels(0)
+        reduce_phase(*chunks[0])
+        for i, (t, c) in enumerate(chunks):
+            if i + 1 < len(chunks):
+                reduce_phase(*chunks[i + 1])
+            features(t, c)
+            if c == CHUNKS - 1:
+                if t > 1:
+                    later_levels(t - 1)
+                first_level(t)
+        for g in range(GROUPS):
+            quantise_wl(g)
+        later_levels(PACK - 1)
 
         a3_bf = keep.tile([P, P3, PACK], BF16, align_bytes=64)
         a3_codes = keep.tile([P, P3], U32, align_bytes=64)

import math
from contextlib import ExitStack

import concourse.mybir as mybir
from concourse.masks import make_identity

T, S, K, H, P1, P2, P3, N = 4096, 2048, 1024, 512, 1024, 512, 256, 1024
FLOPS = 2 * (2 * K * H * S + H * N * P3)

F32 = mybir.dt.float32
BF16 = mybir.dt.bfloat16
I32 = mybir.dt.int32
U32 = mybir.dt.uint32
U16 = mybir.dt.uint16
U8 = mybir.dt.uint8
FP8X4 = mybir.dt.float8_e4m3fn_x4
FP4X4 = mybir.dt.float4_e2m1fn_x4
ALU = mybir.AluOpType
ACT = mybir.ActivationFunctionType

P = 128
PACK = 4
K_PASS = P * PACK
PASSES = K // K_PASS
BANK = 512
CHUNK = 1024
CHUNKS = S // CHUNK
GROUPS = N // K_PASS
TWO_PI = 2.0 * math.pi
MX_BANKS = 4
SUM_BANKS = 4


def tile_list_blind_audition_heats_kernel(
    tc, tab_words, tab_scales, wt, wc_words, wc_scales, gain, wl,
    offs, pos1, pos2, pos3, pos4, pos5, pos6, out_0, out_1, out_2,
):
    nc = tc.nc
    with ExitStack() as ctx:
        keep = ctx.enter_context(tc.tile_pool(name="keep", bufs=1))
        shared = ctx.enter_context(tc.tile_pool(name="shared", bufs=1))
        psum = ctx.enter_context(tc.psum_pool(name="psum", bufs=1))

        def tiles(name, count, shape, dtype):
            return [keep.tile(shape, dtype, align_bytes=64, name=f"{name}{i}") for i in range(count)]

        def load_list(name, src):
            tile = keep.tile(list(src.shape), U16, name=name)
            nc.sync.dma_start(tile[:], src)
            return tile

        offs_sb = load_list("offs_sb", offs)

        scale_win = shared.tile([P, T], U8, offset=32768)
        nc.sync.dma_start(
            scale_win[96:P, :].bitcast(I32),
            tab_scales.bitcast(I32).rearrange("a q w -> q a w"),
        )
        nc.vector.memset(scale_win[0:96, :].bitcast(I32), 0)

        word_win = [shared.tile([P, T], I32, name=f"word_win{a}", offset=a * 4 * T) for a in range(PASSES)]
        wc_raw = keep.tile([P, PASSES, 2 * H], U8)
        wt_raw = [shared.tile([P, PACK, H], F32, name=f"wt_raw{a}", offset=36864 + 8192 * a) for a in range(PASSES)]

        def load_words(a):
            nc.sync.dma_start(word_win[a][:], tab_words[a].rearrange("p t i -> p (t i)").bitcast(I32))

        load_words(0)
        nc.sync.dma_start(wc_raw[:].bitcast(I32), wc_words.bitcast(I32).rearrange("a p w -> p a w"))
        load_words(1)

        zero_in = keep.tile([P, 1], F32)
        zero_bias = keep.tile([P, 1], F32)
        nc.gpsimd.memset(zero_in[:], 0.0)
        nc.scalar.activation(zero_bias[:], zero_in[:], ACT.Silu)

        wcs_raw = shared.tile([P, PASSES, H], U8, offset=36864)
        nc.gpsimd.memset(wcs_raw[:].bitcast(I32), 0)
        for q in range(4):
            nc.scalar.dma_start(
                wcs_raw[32 * q:32 * q + 4].bitcast(I32),
                wc_scales[:, 4 * q:4 * q + 4, :].bitcast(I32).rearrange("a r w -> r a w"),
            )

        v_scales = keep.tile([P, PASSES * S], U8, align_bytes=64)
        nc.gpsimd.memset(v_scales[:].bitcast(I32), 0)
        picked_scales = keep.tile([P, S], U8)
        nc.vector.tensor_copy(picked_scales[:], scale_win[:].indirect(offs_sb[:]))

        wc_planes = shared.tile([P, PASSES, PACK, P], U8, align_bytes=64, offset=32768)
        nc.vector.tensor_copy(
            wc_planes[:].bitcast(I32).rearrange("p a t (q w) -> p a t q w", w=2),
            wcs_raw[:].bitcast(I32).rearrange("p a (q t w) -> p a t q w", t=PACK, w=2),
        )

        def place_scales(q):
            nc.scalar.dma_start(
                v_scales[32 * q:32 * q + 4, :].bitcast(I32),
                picked_scales[96 + 8 * q:96 + 8 * q + 8, :].bitcast(I32),
            )

        place_scales(0)
        for a in range(PASSES):
            nc.sync.dma_start(
                wt_raw[a][:], wt[a * K_PASS:(a + 1) * K_PASS, :].rearrange("(p j) c -> p j c", j=PACK),
            )
        pos = [load_list("pos_sb0", pos1)]
        for q in range(1, 4):
            place_scales(q)
        pos.extend(load_list(f"pos_sb{i + 1}", src) for i, src in enumerate((pos2, pos3, pos4, pos5, pos6)))

        ident = keep.tile([P, P], F32)
        make_identity(nc, ident[:])

        v_words = tiles("v_words", PASSES, [P, S], U32)
        nc.vector.tensor_copy(v_words[0][:], word_win[0][:].bitcast(U32).indirect(offs_sb[:]))

        wc_codes = keep.tile([P, PASSES, PACK, 2 * P], U8, align_bytes=64)
        nc.gpsimd.tensor_copy(
            wc_codes[:].bitcast(I32).rearrange("p a t (q w) -> p a t q w", w=4),
            wc_raw[:].bitcast(I32).rearrange("p a (q t w) -> p a t q w", t=PACK, w=4),
        )
        for s in range(S // BANK):
            nc.vector.tensor_copy(
                v_words[1][:, s * BANK:(s + 1) * BANK],
                word_win[1][:].bitcast(U32).indirect(offs_sb[:, s * BANK // 16:(s + 1) * BANK // 16]),
            )

        wl_raw = shared.tile([P, PACK, N], F32, offset=4096)
        wl_rows = wl.rearrange("(q t s) n -> t q s n", t=PACK, s=8)
        for t in range(PACK):
            nc.sync.dma_start(wl_raw[:, t, :], wl_rows[t])
        gain_col = tiles("gain_col", PACK, [P, 1], F32)
        with nc.allow_non_contiguous_dma(reason="one gain for each partition and row tile"):
            for t in range(PACK):
                nc.sync.dma_start(gain_col[t][:], gain.rearrange("(q t s) -> t q s", t=PACK, s=8)[t])

        wt_bf_first = shared.tile([P, PASSES, P, PACK], BF16, align_bytes=64, offset=27648)
        wt_bf_rest = shared.tile([P, PASSES, P, PACK], BF16, align_bytes=64, offset=28672)
        wt_codes = tiles("wt_codes", PACK, [P, PASSES * P], U32)
        wt_planes = tiles("wt_plane", PACK, [P, PASSES * P], U8)

        def quantise_wt(t):
            rounded = wt_bf_first if t == 0 else wt_bf_rest
            for a in range(PASSES):
                nc.vector.tensor_copy(
                    rounded[:, a].rearrange("p (q s) j -> p q s j", s=8),
                    wt_raw[a][:].rearrange("p j (q t s) -> p t q s j", t=PACK, s=8)[:, t],
                )
            nc.vector.quantize_mx(
                out=wt_codes[t][:].bitcast(FP8X4), scales=wt_planes[t][:],
                in_=rounded[:].rearrange("p a m j -> p (a m j)"),
            )

        banks = [psum.tile([P, BANK], F32, name=f"bank{b}") for b in range(8)]
        mx_turn, sum_turn = [], []

        def next_mx_bank():
            mx_turn.append(0)
            return banks[len(mx_turn) % MX_BANKS]

        def next_sum_bank():
            sum_turn.append(0)
            return banks[MX_BANKS + len(sum_turn) % SUM_BANKS]

        def weights_times_v(codes, planes, s):
            bank = next_mx_bank()
            for a in range(PASSES):
                nc.tensor.matmul_mx(
                    out=bank[:], lhsT=codes[a], lhsT_scale=planes[a],
                    rhs=v_words[a][:, s * BANK:(s + 1) * BANK].bitcast(FP8X4),
                    rhs_scale=v_scales[:, a * S + s * BANK:a * S + (s + 1) * BANK],
                    start=(a == 0), stop=(a == PASSES - 1),
                )
            return bank

        def v_times_wc(t, s):
            bank = next_mx_bank()
            for b in range(BANK // P):
                first = s * BANK + b * P
                for a in range(PASSES):
                    nc.tensor.matmul_mx(
                        out=bank[:, b * P:(b + 1) * P],
                        lhsT=v_words[a][:, first:first + P].bitcast(FP8X4),
                        lhsT_scale=v_scales[:, a * S + first:a * S + first + P],
                        rhs=wc_codes[:, a, t, :].bitcast(FP4X4), rhs_scale=wc_planes[:, a, t, :],
                        start=(a == 0), stop=(a == PASSES - 1),
                    )
            return bank

        cos_buf = tiles("cos_buf", 2 * CHUNKS, [P, CHUNK], F32)
        tanh_buf = tiles("tanh_buf", 2 * CHUNKS, [P, CHUNK], F32)
        angle_buf = tiles("angle_buf", CHUNKS, [P, CHUNK], F32)
        turns_buf = tiles("turns_buf", CHUNKS, [P, CHUNK], U32)
        back_all = shared.tile([P, S], F32, offset=20480)
        back_buf = [back_all[:, c * CHUNK:(c + 1) * CHUNK] for c in range(CHUNKS)]
        h_buf = tiles("h_buf", 2, [P, S], F32)

        def slices(c):
            return [(c * CHUNK // BANK + i, slice(i * BANK, (i + 1) * BANK)) for i in range(CHUNK // BANK)]

        def tanh_tone(t, c):
            codes = [wt_codes[t][:, a * P:(a + 1) * P].bitcast(FP8X4) for a in range(PASSES)]
            planes = [wt_planes[t][:, a * P:(a + 1) * P] for a in range(PASSES)]
            for s, cols in slices(c):
                bank = weights_times_v(codes, planes, s)
                nc.scalar.activation(
                    tanh_buf[(t % 2) * CHUNKS + c][:, cols], bank[:], ACT.Tanh, bias=zero_bias[:],
                )

        def multiply(t, c):
            i = (t % 2) * CHUNKS + c
            nc.vector.tensor_tensor(
                h_buf[t % 2][:, c * CHUNK:(c + 1) * CHUNK], tanh_buf[i][:], cos_buf[i][:], ALU.mult,
            )

        def features_first():
            wc_c = [wc_codes[:, a, 0, :].bitcast(FP4X4) for a in range(PASSES)]
            wc_p = [wc_planes[:, a, 0, :] for a in range(PASSES)]
            wt_c = [wt_codes[0][:, a * P:(a + 1) * P].bitcast(FP8X4) for a in range(PASSES)]
            wt_p = [wt_planes[0][:, a * P:(a + 1) * P] for a in range(PASSES)]
            for c in range(CHUNKS):
                for s, cols in slices(c):
                    bank = weights_times_v(wc_c, wc_p, s)
                    nc.scalar.activation(angle_buf[c][:, cols], bank[:], ACT.Abs)
                    nc.scalar.activation(
                        turns_buf[c][:, cols], angle_buf[c][:, cols], ACT.Copy, scale=1.0 / TWO_PI, bias=-0.25,
                    )
                    nc.vector.scalar_tensor_tensor(
                        back_buf[c][:, cols], turns_buf[c][:, cols].bitcast(I32), -TWO_PI, angle_buf[c][:, cols],
                        ALU.mult, ALU.add,
                    )
            for c in range(CHUNKS):
                for s, cols in slices(c):
                    bank = weights_times_v(wt_c, wt_p, s)
                    nc.scalar.activation(tanh_buf[c][:, cols], bank[:], ACT.Tanh, bias=zero_bias[:])
                    nc.scalar.activation(
                        cos_buf[c][:, cols], back_buf[c][:, cols], ACT.Sin, scale=-1.0, bias=math.pi / 2,
                    )
                    nc.vector.tensor_tensor(
                        h_buf[0][:, s * BANK:(s + 1) * BANK], tanh_buf[c][:, cols], cos_buf[c][:, cols], ALU.mult,
                    )

        sums = {}

        def reduce_phase(t, c):
            angle, back = angle_buf[c], back_buf[c]
            for s, cols in slices(c):
                bank = v_times_wc(t, s)
                nc.scalar.activation(angle[:, cols], bank[:], ACT.Abs)
            turns = turns_buf[c][:]
            nc.scalar.activation(turns, angle[:], ACT.Copy, scale=1.0 / TWO_PI, bias=-0.25)
            nc.scalar.activation(back, turns, ACT.Copy, scale=-TWO_PI)
            for s, cols in slices(c):
                bank = next_sum_bank()
                for b in range(BANK // P):
                    block = slice(cols.start + b * P, cols.start + (b + 1) * P)
                    for part in (angle, back):
                        nc.tensor.matmul(
                            bank[:, b * P:(b + 1) * P], part[:, block], ident[:], is_transpose=True,
                            start=part is angle, stop=part is back,
                        )
                sums[t, s] = bank

        def features(t, c):
            tanh_tone(t, c)
            for s, cols in slices(c):
                nc.scalar.activation(
                    cos_buf[(t % 2) * CHUNKS + c][:, cols], sums[t, s][:], ACT.Sin, scale=-1.0, bias=math.pi / 2,
                )
            multiply(t, c)

        gain_rows = keep.tile([P, PACK, P3], F32)
        a3 = keep.tile([P, PACK, P3], F32)
        left1 = keep.tile([P, P1], F32)
        right1 = keep.tile([P, P1], F32)
        a1 = keep.tile([P, P1], F32)
        a2 = keep.tile([P, P2], F32)

        def halves(n):
            return [(slice(i * n // 2, (i + 1) * n // 2), slice(i * n // 32, (i + 1) * n // 32)) for i in range(2)]

        def first_level(t):
            h = h_buf[t % 2]
            nc.gpsimd.tensor_copy(gain_rows[:, t, :], gain_col[t][:].to_broadcast([P, P3]))
            for cols, lst in halves(P1):
                nc.vector.tensor_copy(left1[:, cols], h[:].indirect(pos[0][:, lst]))
                nc.vector.tensor_copy(right1[:, cols], h[:].indirect(pos[1][:, lst]))
            for cols, lst in halves(P1):
                nc.vector.tensor_tensor(a1[:, cols], left1[:, cols], right1[:, cols], ALU.max)

        def later_levels(t):
            spent = min(t + 1, PACK - 1) % 2 * CHUNKS
            right2, left3 = (tanh_buf[spent], tanh_buf[spent + 1]) if t > 0 else (tanh_buf[0], tanh_buf[1])
            for cols, lst in halves(P2):
                nc.vector.tensor_copy(right2[:, cols], a1[:].indirect(pos[3][:, lst]))
            for cols, lst in halves(P2):
                nc.vector.tensor_tensor(a2[:, cols], a1[:].indirect(pos[2][:, lst]), right2[:, cols], ALU.subtract)
            for cols, lst in halves(P3):
                nc.vector.tensor_tensor(left3[:, cols], a2[:].indirect(pos[4][:, lst]), gain_rows[:, t, cols], ALU.mult)
            for cols, lst in halves(P3):
                nc.vector.tensor_tensor(a3[:, t, cols], a2[:].indirect(pos[5][:, lst]), left3[:, cols], ALU.mult)

        wl_codes = tiles("wl_codes", GROUPS, [P, PACK * P], U32)
        wl_planes = tiles("wl_plane", GROUPS, [P, PACK * P], U8)

        def quantise_wl(g):
            rounded = tanh_buf[CHUNKS + g][:].bitcast(BF16)
            nc.scalar.copy(
                rounded.rearrange("p (u m j) -> p m j u", u=PACK, j=PACK),
                wl_raw[:, :, g * K_PASS:(g + 1) * K_PASS].rearrange("p j (m u) -> p m j u", u=PACK),
            )
            nc.vector.quantize_mx(out=wl_codes[g][:].bitcast(FP8X4), scales=wl_planes[g][:], in_=rounded)

        quantise_wt(0)
        features_first()
        for t in range(1, PACK):
            quantise_wt(t)
        chunks = [(t, c) for t in range(1, PACK) for c in range(CHUNKS)]
        first_level(0)
        later_levels(0)
        reduce_phase(*chunks[0])
        for i, (t, c) in enumerate(chunks):
            if i + 1 < len(chunks):
                reduce_phase(*chunks[i + 1])
            features(t, c)
            if c == CHUNKS - 1:
                if t > 1:
                    later_levels(t - 1)
                first_level(t)
        for g in range(GROUPS):
            quantise_wl(g)
        later_levels(PACK - 1)

        a3_bf = keep.tile([P, P3, PACK], BF16, align_bytes=64)
        a3_codes = keep.tile([P, P3], U32, align_bytes=64)
        a3_plane = keep.tile([P, P3], U8, align_bytes=64)
        for cols, lst in halves(P3):
            nc.vector.tensor_copy(a3_bf[:, cols, :], a3[:, :, cols].rearrange("p t j -> p j t"))
        for cols, lst in halves(P3):
            nc.vector.quantize_mx(
                out=a3_codes[:, cols].bitcast(FP8X4), scales=a3_plane[:, cols],
                in_=a3_bf[:, cols, :].rearrange("p j t -> p (j t)"),
            )

        y = tiles("y", GROUPS, [P, PACK, P3], F32)
        y_bf = tiles("y_bf", GROUPS, [P, P3, PACK], BF16)
        y_codes = keep.tile([P, GROUPS, P3], U32, align_bytes=64)
        y_plane = keep.tile([P, GROUPS, P3], U8, align_bytes=64)
        for i, (cols, lst) in enumerate(halves(P3)):
            for g in range(GROUPS):
                bank = banks[i * GROUPS + g]
                for u in range(PACK):
                    nc.tensor.matmul_mx(
                        out=bank[:, u * P:(u + 1) * P],
                        lhsT=wl_codes[g][:, u * P:(u + 1) * P].bitcast(FP8X4),
                        lhsT_scale=wl_planes[g][:, u * P:(u + 1) * P],
                        rhs=a3_codes[:, cols].bitcast(FP8X4), rhs_scale=a3_plane[:, cols],
                        start=True, stop=True,
                    )
                nc.scalar.copy(y[g][:, :, cols], bank[:].rearrange("p (u m) -> p u m", u=PACK))
                nc.vector.tensor_copy(y_bf[g][:, cols, :], y[g][:, :, cols].rearrange("p u m -> p m u"))
                nc.vector.quantize_mx(
                    out=y_codes[:, g, cols].bitcast(FP8X4), scales=y_plane[:, g, cols],
                    in_=y_bf[g][:, cols, :].rearrange("p m u -> p (m u)"),
                )
        for g in range(GROUPS):
            nc.sync.dma_start(out_0[g * K_PASS:(g + 1) * K_PASS, :].rearrange("(p u) m -> p u m", u=PACK), y[g][:])
        for g in range(GROUPS):
            nc.sync.dma_start(
                out_1[g].rearrange("p m i -> p (m i)").bitcast(I32), y_codes[:, g, :].bitcast(I32),
            )
        for q in range(4):
            queue = nc.sync if q % 2 == 0 else nc.scalar
            queue.dma_start(
                out_2[:, 4 * q:4 * q + 4, :].bitcast(I32).rearrange("g r w -> r g w"),
                y_plane[32 * q:32 * q + 4].bitcast(I32),
            )
